import numpy as np, ml_dtypes
CORES = [1,3,5,9,11,13]
N = 6
import mx_ref
NC, G, MB, ROOT = 128, 4, 4, 2
C = np.float32(0.041)
BF = ml_dtypes.bfloat16
def cut(t, i, w=512):
    return t[:, w * i:w * i + w]
def tile(rs):
    return np.stack(rs, axis=2).reshape(128, -1).astype(BF)
def layer(w, X):
    out = []
    for i in range(G):
        for t in range(len(X)):
            p = mx_ref.matmul(mx_ref.quantize(cut(w, len(X) * i + t)), X[t])
            z = p if t == 0 else z + p
        out.append(z)
    return out
def act(Z):
    return [np.maximum(z, 0) * C for z in Z]
def setup_inputs(rng):
    def f(*shape):
        return mx_ref.flush((rng.standard_normal(shape, dtype=np.float32) * np.exp2(rng.integers(-2, 3, shape[:-1] + (1,)))).astype(BF))
    return {"x": f(N, 128, MB * 4 * NC), "w1": f(N, 128, G * 512), "w2": f(N, 128, 512)}
def setup_inputs_blocks(rng):
    d = setup_inputs(rng)
    for k in ("x", "w1", "w2"): d[k] = mx_ref.spread(d[k], rng, 4)
    return d
def setup_inputs_wide(rng):
    d = setup_inputs(rng)
    for k in ("x", "w1", "w2"): d[k] = mx_ref.flush((d[k].astype(np.float32) * np.exp2(rng.integers(-8, 9, (N, 1, 1))).astype(np.float32)).astype(BF))
    return d
def setup_inputs_zeros(rng):
    d = setup_inputs(rng); v = d["x"].reshape(N, 128, -1, 4).copy()
    v[np.broadcast_to((rng.random((N, 1, v.shape[2], 1)) < 0.33), v.shape)] = 0
    d["x"] = v.reshape(d["x"].shape)
    return d
def reference(x, w1, w2):
    H = [mx_ref.quantize(tile(act(layer(w1[ROOT], [mx_ref.quantize(cut(x[ROOT], m, 4 * NC))])))) for m in range(MB)]
    y = np.zeros((N, 128, MB * NC), np.float32)
    for r in range(N):
        qw = mx_ref.quantize(w2[r])
        for m in range(MB):
            y[r][:, NC * m:NC * m + NC] = mx_ref.matmul(qw, H[m])
    return {"y": y}

@@ -1,0 +1,211 @@
+import numpy as np
+from concourse.bass import DstId, RemoteDMATransfer
+from concourse.mybir import dt, AluOpType, ActivationFunctionType
+
+SIM_CORES = 16
+NCOL = 512
+STEPS = [(0, 192), (192, 384), (384, 512)]
+SCALE = float(np.float32(0.041))
+
+SCRATCH = {
+    "xb": ("sbuf", [128, 4 * NCOL], "bfloat16"),
+    "w1b": ("sbuf", [128, 4 * 512], "bfloat16"),
+    "w2b": ("sbuf", [128, 512], "bfloat16"),
+    "hb": ("sbuf", [128, 4 * NCOL], "bfloat16"),
+    "xq": ("sbuf", [128, NCOL], "float8_e4m3fn_x4"),
+    "xs": ("sbuf", [128, NCOL], "uint8"),
+    "w1q": ("sbuf", [128, 512], "float8_e4m3fn_x4"),
+    "w1s": ("sbuf", [128, 512], "uint8"),
+    "w2q": ("sbuf", [128, 128], "float8_e4m3fn_x4"),
+    "w2s": ("sbuf", [128, 128], "uint8"),
+    "hq": ("sbuf", [128, NCOL], "float8_e4m3fn_x4"),
+    "hs": ("sbuf", [128, NCOL], "uint8"),
+    "yb": ("sbuf", [128, NCOL], "float32"),
+    "ps": ("psum", [128, 8 * 512], "float32"),
+}
+SEMAPHORES = (["lw1", "lw2", "lx0", "lx1", "lx2", "qwa", "qwb", "qw2", "qx0", "qx1", "qx2"]
+              + ["z%d%d" % (s, b) for s in range(3) for b in range(4)]
+              + ["act0", "act1", "act2", "qh0", "qh1", "qh2"]
+              + ["zy0", "zy1", "cy", "st", "hop", "arr", "sent"])
+
+
+def bits(mask):
+    return [b for b in range(mask.bit_length()) if (mask >> b) & 1]
+
+
+def to_mask(engines):
+    return sum(1 << b for b in engines)
+
+
+def relays_of(T, topo):
+    root = T.cores[T.root]
+    away = [c for c in T.cores if topo.chip(c) != topo.chip(root)]
+    own = [c for c in range(SIM_CORES) if c != root and topo.chip(c) == topo.chip(root)
+           and all(topo.may_write(c, d) for d in away)]
+    own.sort(key=lambda c: (T.rank_of(c) is None, c))
+    far = [c for c in own if topo.die(c) != topo.die(root)]
+    near = [c for c in own if topo.die(c) == topo.die(root)]
+    return [far[0], near[0], far[1], near[1]]
+
+
+def piece(T, k):
+    if k == 3:
+        return T.hs[:, 0:NCOL]
+    a, b = STEPS[k]
+    return T.hq[:, a:b].bitcast(dt.uint8)
+
+
+def dst_id(topo, c):
+    rid, pid, _ = topo.addr(c)
+    return DstId(rid=rid, pnc=pid)
+
+
+def second_layer(g, T, ready):
+    half = NCOL // 2
+    g.tensor.wait_ge(T.sem.qw2, 1)
+    for s, n in ready:
+        g.tensor.wait_ge(s, n)
+    for i in range(2):
+        a = half * i
+        o = 512 * (4 + i)
+        g.tensor.matmul_mx(T.ps[:, o:o + half], T.w2q[:, 0:128], T.w2s[:, 0:128],
+                           T.hq[:, a:a + half], T.hs[:, a:a + half], True, True).then_inc(T.sem["zy%d" % i], 1)
+    g.vector.wait_ge(T.sem.zy0, 1)
+    g.vector.tensor_copy(T.yb[:, 0:half], T.ps[:, 2048:2048 + half]).then_inc(T.sem.cy, 1)
+    g.scalar.wait_ge(T.sem.zy1, 1)
+    g.scalar.activation(T.yb[:, half:NCOL], T.ps[:, 2560:2560 + half], ActivationFunctionType.Copy).then_inc(T.sem.cy, 1)
+    g.sync.wait_ge(T.sem.cy, 2)
+    g.sync.dma_start(T.y[:, :], T.yb[:, :]).then_inc(T.sem.st, 16)
+    g.sync.wait_ge(T.sem.st, 16)
+
+
+def root_program(g, core, T, topo):
+    S = T.sem
+    g.sync.dma_start(T.w1b[:, :], T.w1[:, :]).then_inc(S.lw1, 16)
+    for s, q in ((0, g.scalar), (1, g.sync), (2, g.scalar)):
+        a, b = STEPS[s]
+        q.dma_start(T.xb[:, 4 * a:4 * b], T.x[:, 4 * a:4 * b]).then_inc(S["lx%d" % s], 16)
+    g.sync.dma_start(T.w2b[:, :], T.w2[:, :]).then_inc(S.lw2, 16)
+
+    def quant_x(s):
+        a, b = STEPS[s]
+        g.vector.wait_ge(S["lx%d" % s], 16)
+        g.vector.quantize_mx(T.xq[:, a:b], T.xs[:, a:b], T.xb[:, 4 * a:4 * b]).then_inc(S["qx%d" % s], 1)
+
+    def bank(s, b):
+        return 512 * (4 * (s % 2) + b)
+
+    def products(s):
+        a, e = STEPS[s]
+        g.tensor.wait_ge(S["qx%d" % s], 1)
+        if s >= 2:
+            g.tensor.wait_ge(S["act%d" % (s - 2)], 4)
+        for b in range(4):
+            if s == 0 and b == 0:
+                g.tensor.wait_ge(S.qwa, 1)
+            if s == 0 and b == 2:
+                g.tensor.wait_ge(S.qwb, 1)
+            o = bank(s, b)
+            g.tensor.matmul_mx(T.ps[:, o:o + e - a], T.w1q[:, 128 * b:128 * b + 128], T.w1s[:, 128 * b:128 * b + 128],
+                               T.xq[:, a:e], T.xs[:, a:e], True, True).then_inc(S["z%d%d" % (s, b)], 1)
+
+    def on_scalar(s, b):
+        a, e = STEPS[s]
+        o = bank(s, b)
+        g.scalar.wait_ge(S["z%d%d" % (s, b)], 1)
+        g.scalar.activation(T.hb[:, 4 * a + b:4 * e:4], T.ps[:, o:o + e - a], ActivationFunctionType.Relu,
+                            scale=SCALE).then_inc(S["act%d" % s], 1)
+
+    def on_vector(s, b):
+        a, e = STEPS[s]
+        o = bank(s, b)
+        g.vector.wait_ge(S["z%d%d" % (s, b)], 1)
+        g.vector.tensor_scalar(T.hb[:, 4 * a + b:4 * e:4], T.ps[:, o:o + e - a], 0.0, SCALE,
+                               AluOpType.max, AluOpType.mult).then_inc(S["act%d" % s], 1)
+
+    def quant_h(s):
+        a, b = STEPS[s]
+        g.vector.wait_ge(S["act%d" % s], 4)
+        g.vector.quantize_mx(T.hq[:, a:b], T.hs[:, a:b], T.hb[:, 4 * a:4 * b]).then_inc(S["qh%d" % s], 1)
+
+    g.vector.wait_ge(S.lw1, 16)
+    g.vector.quantize_mx(T.w1q[:, 0:256], T.w1s[:, 0:256], T.w1b[:, 0:1024]).then_inc(S.qwa, 1)
+    g.vector.quantize_mx(T.w1q[:, 256:512], T.w1s[:, 256:512], T.w1b[:, 1024:2048]).then_inc(S.qwb, 1)
+    quant_x(0)
+    quant_x(1)
+    on_vector(0, 3)
+    quant_h(0)
+    quant_x(2)
+    on_vector(1, 3)
+    quant_h(1)
+    on_vector(2, 1)
+    on_vector(2, 3)
+    quant_h(2)
+    g.vector.wait_ge(S.lw2, 16)
+    g.vector.quantize_mx(T.w2q[:, 0:128], T.w2s[:, 0:128], T.w2b[:, 0:512]).then_inc(S.qw2, 1)
+    for s, b in ((0, 0), (0, 1), (0, 2), (1, 0), (1, 1), (1, 2), (2, 0), (2, 2)):
+        on_scalar(s, b)
+    for s in range(3):
+        products(s)
+
+    relay = relays_of(T, topo)
+    eng = bits(topo.mask(core, relay[0]))
+    lanes = [to_mask(eng[0::2]), to_mask(eng[1::2])]
+
+    def to_relay(k):
+        return RemoteDMATransfer(dst_ids=[dst_id(topo, relay[k])], dma_engine_mask=lanes[k % 2], remote_sem=S.hop,
+                                 srcs=[piece(T, k)], dsts=[piece(T, k)])
+
+    g.wait_ge(S.qh0, 1)
+    g.remote_dma_fused([to_relay(0)], local_sem=S.sent)
+    g.wait_ge(S.qh1, 1)
+    g.remote_dma_fused([to_relay(1)], local_sem=S.sent)
+    g.wait_ge(S.qh2, 1)
+    g.remote_dma_fused([to_relay(2), to_relay(3)], local_sem=S.sent)
+    g.wait_ge(S.sent, 2 * len(eng))
+
+    second_layer(g, T, [(S.qh0, 1), (S.qh1, 1), (S.qh2, 1), (S.act1, 4)])
+
+
+def rank_program(g, core, T, topo):
+    root = T.cores[T.root]
+    if core == root:
+        root_program(g, core, T, topo)
+        return
+    relay = relays_of(T, topo)
+    rank = T.rank_of(core)
+    lane = len(bits(topo.mask(root, relay[0]))) // 2
+
+    if rank is not None:
+        g.sync.dma_start(T.w2b[:, :], T.w2[:, :]).then_inc(T.sem.lw2, 16)
+        g.vector.wait_ge(T.sem.lw2, 16)
+        g.vector.quantize_mx(T.w2q[:, 0:128], T.w2s[:, 0:128], T.w2b[:, 0:512]).then_inc(T.sem.qw2, 1)
+
+    if core in relay:
+        k = relay.index(core)
+        away = [c for c in T.cores if topo.chip(c) != topo.chip(core)]
+        here = [c for c in T.cores if topo.chip(c) == topo.chip(core) and c not in (core, root)]
+        out = topo.mask(core, away[0])
+        rest = topo.mask(core, here[0]) & ~out
+        sent = 0
+        g.wait_ge(T.sem.hop, lane)
+        for dsts, mask in ((away, out), (here, rest)):
+            g.remote_dma_fused([RemoteDMATransfer(dst_ids=[dst_id(topo, c) for c in dsts], dma_engine_mask=mask,
+                                                  remote_sem=T.sem.arr, srcs=[piece(T, k)],
+                                                  dsts=[piece(T, k) for c in dsts])], local_sem=T.sem.sent)
+            sent += len(bits(mask))
+        g.wait_ge(T.sem.sent, sent)
+
+    if rank is not None:
+        n = 0
+        for r in relay:
+            if r == core:
+                continue
+            m = topo.mask(r, core)
+            if topo.chip(r) == topo.chip(core):
+                m &= ~topo.mask(r, [c for c in T.cores if topo.chip(c) != topo.chip(r)][0])
+            n += len(bits(m))
+        ready = [(T.sem.arr, n)]
+        if core in relay:
+            ready.append((T.sem.hop, lane))
+        second_layer(g, T, ready)

@@ -4,8 +4,26 @@ from concourse.mybir import dt, AluOpType, ActivationFunctionType
 
 SIM_CORES = 16
 NCOL = 512
-STEPS = [(0, 192), (192, 384), (384, 512)]
+STEPS = [(0, 128), (128, 256), (256, 384), (384, 512)]
+ON_VECTOR = [(2, 3), (3,), (3,), (1, 3)]
 SCALE = float(np.float32(0.041))
+HOME = "home"
+
+SENDS = [
+    [("hq", 0, 128, 3, (0, 1, HOME))],
+    [("hq", 0, 64, 2, (2,)), ("hq", 64, 128, 1, (2,))],
+    [("hq", 128, 256, 0, (0, 1, 2, HOME))],
+    [("hq", 256, 384, 2, (0, 1, 2, HOME))],
+    [("hs", 0, 512, 1, (0, 2, HOME))],
+    [("hq", 384, 512, 2, (1,)), ("hs", 0, 512, 3, (1,))],
+    [("hq", 384, 512, 1, (0,))],
+    [("hq", 384, 512, 3, (2,))],
+    [("hq", 384, 512, None, (HOME,))],
+]
+PIECES = [p for call in SENDS for p in call]
+Y_PARTS = [(0, 192), (192, 384), (384, 512)]
+Y_EARLY = [(0, 384), (384, 512)]
+Y_WHOLE = [(0, 512)]
 
 SCRATCH = {
     "xb": ("sbuf", [128, 4 * NCOL], "bfloat16"),
@@ -23,10 +41,11 @@ SCRATCH = {
     "yb": ("sbuf", [128, NCOL], "float32"),
     "ps": ("psum", [128, 8 * 512], "float32"),
 }
-SEMAPHORES = (["lw1", "lw2", "lx0", "lx1", "lx2", "qwa", "qwb", "qw2", "qx0", "qx1", "qx2"]
-              + ["z%d%d" % (s, b) for s in range(3) for b in range(4)]
-              + ["act0", "act1", "act2", "qh0", "qh1", "qh2"]
-              + ["zy0", "zy1", "cy", "st", "hop", "arr", "sent"])
+SEMAPHORES = (["lw1", "lw2", "qwa", "qwb", "qw2", "sent"]
+              + ["%s%d" % (n, s) for n in ("lx", "qx", "act", "qh") for s in range(len(STEPS))]
+              + ["z%d%d" % (s, b) for s in range(len(STEPS)) for b in range(4)]
+              + ["%s%d" % (n, i) for n in ("zy", "cy", "st") for i in range(len(Y_PARTS))]
+              + ["%s%d" % (n, k) for n in ("hop", "arr") for k in range(len(PIECES))])
 
 
 def bits(mask):
@@ -37,66 +56,82 @@ def to_mask(engines):
     return sum(1 << b for b in engines)
 
 
-def relays_of(T, topo):
+def plan(T, topo):
     root = T.cores[T.root]
     away = [c for c in T.cores if topo.chip(c) != topo.chip(root)]
+    home = [c for c in T.cores if topo.chip(c) == topo.chip(root) and c != root]
     own = [c for c in range(SIM_CORES) if c != root and topo.chip(c) == topo.chip(root)
            and all(topo.may_write(c, d) for d in away)]
     own.sort(key=lambda c: (T.rank_of(c) is None, c))
     far = [c for c in own if topo.die(c) != topo.die(root)]
     near = [c for c in own if topo.die(c) == topo.die(root)]
-    return [far[0], near[0], far[1], near[1]]
+    return [far[0], near[0], far[1], near[1]], away, home
 
 
-def piece(T, k):
-    if k == 3:
-        return T.hs[:, 0:NCOL]
-    a, b = STEPS[k]
-    return T.hq[:, a:b].bitcast(dt.uint8)
+def view(T, p):
+    v = T[p[0]][:, p[1]:p[2]]
+    return v.bitcast(dt.uint8) if p[0] == "hq" else v
 
 
-def dst_id(topo, c):
-    rid, pid, _ = topo.addr(c)
-    return DstId(rid=rid, pnc=pid)
+def transfer(T, topo, p, cores, mask, sem):
+    ids = [DstId(rid=topo.addr(c)[0], pnc=topo.addr(c)[1]) for c in cores]
+    return RemoteDMATransfer(dst_ids=ids, dma_engine_mask=mask, remote_sem=sem, srcs=[view(T, p)],
+                             dsts=[view(T, p) for c in cores])
 
 
-def second_layer(g, T, ready):
-    half = NCOL // 2
-    g.tensor.wait_ge(T.sem.qw2, 1)
-    for s, n in ready:
-        g.tensor.wait_ge(s, n)
-    for i in range(2):
-        a = half * i
+def root_masks(T, topo):
+    root = T.cores[T.root]
+    eng = bits(topo.mask(root, plan(T, topo)[0][0]))
+    return [to_mask(eng[i::len(call)]) for call in SENDS for i in range(len(call))]
+
+
+def relay_masks(T, topo):
+    relay, away, home = plan(T, topo)
+    out = topo.mask(relay[0], away[0])
+    return out, topo.mask(relay[0], T.cores[T.root]) & ~out
+
+
+def second_layer(g, T, needs, stores):
+    S = T.sem
+    g.tensor.wait_ge(S.qw2, 1)
+    for i, (a, b) in enumerate(Y_PARTS):
+        for s, n in needs(a, b):
+            g.tensor.wait_ge(s, n)
         o = 512 * (4 + i)
-        g.tensor.matmul_mx(T.ps[:, o:o + half], T.w2q[:, 0:128], T.w2s[:, 0:128],
-                           T.hq[:, a:a + half], T.hs[:, a:a + half], True, True).then_inc(T.sem["zy%d" % i], 1)
-    g.vector.wait_ge(T.sem.zy0, 1)
-    g.vector.tensor_copy(T.yb[:, 0:half], T.ps[:, 2048:2048 + half]).then_inc(T.sem.cy, 1)
-    g.scalar.wait_ge(T.sem.zy1, 1)
-    g.scalar.activation(T.yb[:, half:NCOL], T.ps[:, 2560:2560 + half], ActivationFunctionType.Copy).then_inc(T.sem.cy, 1)
-    g.sync.wait_ge(T.sem.cy, 2)
-    g.sync.dma_start(T.y[:, :], T.yb[:, :]).then_inc(T.sem.st, 16)
-    g.sync.wait_ge(T.sem.st, 16)
+        g.tensor.matmul_mx(T.ps[:, o:o + b - a], T.w2q[:, 0:128], T.w2s[:, 0:128],
+                           T.hq[:, a:b], T.hs[:, a:b], True, True).then_inc(S["zy%d" % i], 1)
+        k = [j for j, (u, v) in enumerate(stores) if u <= a and b <= v][0]
+        if i % 2 == 0:
+            g.vector.wait_ge(S["zy%d" % i], 1)
+            g.vector.tensor_copy(T.yb[:, a:b], T.ps[:, o:o + b - a]).then_inc(S["cy%d" % k], 1)
+        else:
+            g.scalar.wait_ge(S["zy%d" % i], 1)
+            g.scalar.activation(T.yb[:, a:b], T.ps[:, o:o + b - a],
+                                ActivationFunctionType.Copy).then_inc(S["cy%d" % k], 1)
+    for k, (u, v) in enumerate(stores):
+        g.sync.wait_ge(S["cy%d" % k], len([1 for a, b in Y_PARTS if u <= a and b <= v]))
+        g.sync.dma_start(T.y[:, u:v], T.yb[:, u:v]).then_inc(S["st%d" % k], 16)
+    for k in range(len(stores)):
+        g.sync.wait_ge(S["st%d" % k], 16)
 
 
 def root_program(g, core, T, topo):
     S = T.sem
     g.sync.dma_start(T.w1b[:, :], T.w1[:, :]).then_inc(S.lw1, 16)
-    for s, q in ((0, g.scalar), (1, g.sync), (2, g.scalar)):
-        a, b = STEPS[s]
+    for s, (a, b) in enumerate(STEPS):
+        q = g.scalar if s in (0, 2) else g.sync
         q.dma_start(T.xb[:, 4 * a:4 * b], T.x[:, 4 * a:4 * b]).then_inc(S["lx%d" % s], 16)
     g.sync.dma_start(T.w2b[:, :], T.w2[:, :]).then_inc(S.lw2, 16)
+
+    def bank(s, b):
+        return 512 * (4 * (s % 2) + b)
 
     def quant_x(s):
         a, b = STEPS[s]
         g.vector.wait_ge(S["lx%d" % s], 16)
         g.vector.quantize_mx(T.xq[:, a:b], T.xs[:, a:b], T.xb[:, 4 * a:4 * b]).then_inc(S["qx%d" % s], 1)
 
-    def bank(s, b):
-        return 512 * (4 * (s % 2) + b)
-
-    def products(s):
-        a, e = STEPS[s]
+    for s, (a, e) in enumerate(STEPS):
         g.tensor.wait_ge(S["qx%d" % s], 1)
         if s >= 2:
             g.tensor.wait_ge(S["act%d" % (s - 2)], 4)
@@ -109,62 +144,53 @@ def root_program(g, core, T, topo):
             g.tensor.matmul_mx(T.ps[:, o:o + e - a], T.w1q[:, 128 * b:128 * b + 128], T.w1s[:, 128 * b:128 * b + 128],
                                T.xq[:, a:e], T.xs[:, a:e], True, True).then_inc(S["z%d%d" % (s, b)], 1)
 
-    def on_scalar(s, b):
-        a, e = STEPS[s]
-        o = bank(s, b)
-        g.scalar.wait_ge(S["z%d%d" % (s, b)], 1)
-        g.scalar.activation(T.hb[:, 4 * a + b:4 * e:4], T.ps[:, o:o + e - a], ActivationFunctionType.Relu,
-                            scale=SCALE).then_inc(S["act%d" % s], 1)
-
-    def on_vector(s, b):
-        a, e = STEPS[s]
-        o = bank(s, b)
-        g.vector.wait_ge(S["z%d%d" % (s, b)], 1)
-        g.vector.tensor_scalar(T.hb[:, 4 * a + b:4 * e:4], T.ps[:, o:o + e - a], 0.0, SCALE,
-                               AluOpType.max, AluOpType.mult).then_inc(S["act%d" % s], 1)
-
-    def quant_h(s):
-        a, b = STEPS[s]
-        g.vector.wait_ge(S["act%d" % s], 4)
-        g.vector.quantize_mx(T.hq[:, a:b], T.hs[:, a:b], T.hb[:, 4 * a:4 * b]).then_inc(S["qh%d" % s], 1)
+    for s, (a, e) in enumerate(STEPS):
+        for b in range(4):
+            if b not in ON_VECTOR[s]:
+                o = bank(s, b)
+                g.scalar.wait_ge(S["z%d%d" % (s, b)], 1)
+                g.scalar.activation(T.hb[:, 4 * a + b:4 * e:4], T.ps[:, o:o + e - a], ActivationFunctionType.Relu,
+                                    scale=SCALE).then_inc(S["act%d" % s], 1)
 
     g.vector.wait_ge(S.lw1, 16)
     g.vector.quantize_mx(T.w1q[:, 0:256], T.w1s[:, 0:256], T.w1b[:, 0:1024]).then_inc(S.qwa, 1)
     g.vector.quantize_mx(T.w1q[:, 256:512], T.w1s[:, 256:512], T.w1b[:, 1024:2048]).then_inc(S.qwb, 1)
     quant_x(0)
     quant_x(1)
-    on_vector(0, 3)
-    quant_h(0)
-    quant_x(2)
-    on_vector(1, 3)
-    quant_h(1)
-    on_vector(2, 1)
-    on_vector(2, 3)
-    quant_h(2)
+    for s, (a, e) in enumerate(STEPS):
+        for b in ON_VECTOR[s]:
+            o = bank(s, b)
+            g.vector.wait_ge(S["z%d%d" % (s, b)], 1)
+            g.vector.tensor_scalar(T.hb[:, 4 * a + b:4 * e:4], T.ps[:, o:o + e - a], 0.0, SCALE,
+                                   AluOpType.max, AluOpType.mult).then_inc(S["act%d" % s], 1)
+        g.vector.wait_ge(S["act%d" % s], 4)
+        g.vector.quantize_mx(T.hq[:, a:e], T.hs[:, a:e], T.hb[:, 4 * a:4 * e]).then_inc(S["qh%d" % s], 1)
+        if s + 2 < len(STEPS):
+            quant_x(s + 2)
     g.vector.wait_ge(S.lw2, 16)
     g.vector.quantize_mx(T.w2q[:, 0:128], T.w2s[:, 0:128], T.w2b[:, 0:512]).then_inc(S.qw2, 1)
-    for s, b in ((0, 0), (0, 1), (0, 2), (1, 0), (1, 1), (1, 2), (2, 0), (2, 2)):
-        on_scalar(s, b)
-    for s in range(3):
-        products(s)
 
-    relay = relays_of(T, topo)
-    eng = bits(topo.mask(core, relay[0]))
-    lanes = [to_mask(eng[0::2]), to_mask(eng[1::2])]
+    relay, away, home = plan(T, topo)
+    masks = root_masks(T, topo)
+    packed = 0
+    k = 0
+    for call in SENDS:
+        last = max(p[2] for p in call)
+        while packed < len(STEPS) and STEPS[packed][0] < last:
+            g.wait_ge(S["qh%d" % packed], 1)
+            packed += 1
+        parts = []
+        for p in call:
+            if p[3] is None:
+                parts.append(transfer(T, topo, p, home, masks[k], S["arr%d" % k]))
+            else:
+                parts.append(transfer(T, topo, p, [relay[p[3]]], masks[k], S["hop%d" % k]))
+            k += 1
+        g.remote_dma_fused(parts, local_sem=S.sent)
+    g.wait_ge(S.sent, sum(len(bits(m)) for m in masks))
 
-    def to_relay(k):
-        return RemoteDMATransfer(dst_ids=[dst_id(topo, relay[k])], dma_engine_mask=lanes[k % 2], remote_sem=S.hop,
-                                 srcs=[piece(T, k)], dsts=[piece(T, k)])
-
-    g.wait_ge(S.qh0, 1)
-    g.remote_dma_fused([to_relay(0)], local_sem=S.sent)
-    g.wait_ge(S.qh1, 1)
-    g.remote_dma_fused([to_relay(1)], local_sem=S.sent)
-    g.wait_ge(S.qh2, 1)
-    g.remote_dma_fused([to_relay(2), to_relay(3)], local_sem=S.sent)
-    g.wait_ge(S.sent, 2 * len(eng))
-
-    second_layer(g, T, [(S.qh0, 1), (S.qh1, 1), (S.qh2, 1), (S.act1, 4)])
+    second_layer(g, T, lambda a, b: [(S["%s%d" % (n, s)], c) for s in range(len(STEPS)) for n, c in (("qh", 1), ("act", 4))],
+                 Y_WHOLE)
 
 
 def rank_program(g, core, T, topo):
@@ -172,40 +198,43 @@ def rank_program(g, core, T, topo):
     if core == root:
         root_program(g, core, T, topo)
         return
-    relay = relays_of(T, topo)
+    S = T.sem
+    relay, away, home = plan(T, topo)
+    masks = root_masks(T, topo)
+    out, rest = relay_masks(T, topo)
     rank = T.rank_of(core)
-    lane = len(bits(topo.mask(root, relay[0]))) // 2
 
     if rank is not None:
-        g.sync.dma_start(T.w2b[:, :], T.w2[:, :]).then_inc(T.sem.lw2, 16)
-        g.vector.wait_ge(T.sem.lw2, 16)
-        g.vector.quantize_mx(T.w2q[:, 0:128], T.w2s[:, 0:128], T.w2b[:, 0:512]).then_inc(T.sem.qw2, 1)
+        g.sync.dma_start(T.w2b[:, :], T.w2[:, :]).then_inc(S.lw2, 16)
+        g.vector.wait_ge(S.lw2, 16)
+        g.vector.quantize_mx(T.w2q[:, 0:128], T.w2s[:, 0:128], T.w2b[:, 0:512]).then_inc(S.qw2, 1)
 
     if core in relay:
-        k = relay.index(core)
-        away = [c for c in T.cores if topo.chip(c) != topo.chip(core)]
-        here = [c for c in T.cores if topo.chip(c) == topo.chip(core) and c not in (core, root)]
-        out = topo.mask(core, away[0])
-        rest = topo.mask(core, here[0]) & ~out
         sent = 0
-        g.wait_ge(T.sem.hop, lane)
-        for dsts, mask in ((away, out), (here, rest)):
-            g.remote_dma_fused([RemoteDMATransfer(dst_ids=[dst_id(topo, c) for c in dsts], dma_engine_mask=mask,
-                                                  remote_sem=T.sem.arr, srcs=[piece(T, k)],
-                                                  dsts=[piece(T, k) for c in dsts])], local_sem=T.sem.sent)
-            sent += len(bits(mask))
-        g.wait_ge(T.sem.sent, sent)
+        for k, p in enumerate(PIECES):
+            if p[3] is None or relay[p[3]] != core:
+                continue
+            g.wait_ge(S["hop%d" % k], len(bits(masks[k])))
+            there = [away[d] for d in p[4] if d != HOME]
+            here = [c for c in home if c != core] if HOME in p[4] else []
+            for cores, mask in ((there, out), (here, rest)):
+                if cores:
+                    g.remote_dma_fused([transfer(T, topo, p, cores, mask, S["arr%d" % k])], local_sem=S.sent)
+                    sent += len(bits(mask))
+        g.wait_ge(S.sent, sent)
 
     if rank is not None:
-        n = 0
-        for r in relay:
-            if r == core:
-                continue
-            m = topo.mask(r, core)
-            if topo.chip(r) == topo.chip(core):
-                m &= ~topo.mask(r, [c for c in T.cores if topo.chip(c) != topo.chip(r)][0])
-            n += len(bits(m))
-        ready = [(T.sem.arr, n)]
-        if core in relay:
-            ready.append((T.sem.hop, lane))
-        second_layer(g, T, ready)
+        def needs(a, b):
+            r = []
+            for k, p in enumerate(PIECES):
+                if p[1] >= b or p[2] <= a:
+                    continue
+                if p[3] is not None and relay[p[3]] == core:
+                    if HOME in p[4]:
+                        r.append((S["hop%d" % k], len(bits(masks[k]))))
+                elif core in away and away.index(core) in p[4]:
+                    r.append((S["arr%d" % k], len(bits(out))))
+                elif core in home and HOME in p[4]:
+                    r.append((S["arr%d" % k], len(bits(masks[k] if p[3] is None else rest))))
+            return r
+        second_layer(g, T, needs, Y_WHOLE if core in relay else Y_EARLY)

import numpy as np
from concourse.bass import DstId, RemoteDMATransfer
from concourse.mybir import dt, AluOpType, ActivationFunctionType

SIM_CORES = 16
NCOL = 512
STEPS = [(0, 128), (128, 256), (256, 384), (384, 512)]
ON_VECTOR = [(2, 3), (3,), (3,), (1, 3)]
SCALE = float(np.float32(0.041))
HOME = "home"

SENDS = [
    [("hq", 0, 128, 3, (0, 1, HOME))],
    [("hq", 0, 64, 2, (2,)), ("hq", 64, 128, 1, (2,))],
    [("hq", 128, 256, 0, (0, 1, 2, HOME))],
    [("hq", 256, 384, 2, (0, 1, 2, HOME))],
    [("hs", 0, 512, 1, (0, 2, HOME))],
    [("hq", 384, 512, 2, (1,)), ("hs", 0, 512, 3, (1,))],
    [("hq", 384, 512, 1, (0,))],
    [("hq", 384, 512, 3, (2,))],
    [("hq", 384, 512, None, (HOME,))],
]
PIECES = [p for call in SENDS for p in call]
Y_PARTS = [(0, 192), (192, 384), (384, 512)]
Y_EARLY = [(0, 384), (384, 512)]
Y_WHOLE = [(0, 512)]

SCRATCH = {
    "xb": ("sbuf", [128, 4 * NCOL], "bfloat16"),
    "w1b": ("sbuf", [128, 4 * 512], "bfloat16"),
    "w2b": ("sbuf", [128, 512], "bfloat16"),
    "hb": ("sbuf", [128, 4 * NCOL], "bfloat16"),
    "xq": ("sbuf", [128, NCOL], "float8_e4m3fn_x4"),
    "xs": ("sbuf", [128, NCOL], "uint8"),
    "w1q": ("sbuf", [128, 512], "float8_e4m3fn_x4"),
    "w1s": ("sbuf", [128, 512], "uint8"),
    "w2q": ("sbuf", [128, 128], "float8_e4m3fn_x4"),
    "w2s": ("sbuf", [128, 128], "uint8"),
    "hq": ("sbuf", [128, NCOL], "float8_e4m3fn_x4"),
    "hs": ("sbuf", [128, NCOL], "uint8"),
    "yb": ("sbuf", [128, NCOL], "float32"),
    "ps": ("psum", [128, 8 * 512], "float32"),
}
SEMAPHORES = (["lw1", "lw2", "qwa", "qwb", "qw2", "sent"]
              + ["%s%d" % (n, s) for n in ("lx", "qx", "act", "qh") for s in range(len(STEPS))]
              + ["z%d%d" % (s, b) for s in range(len(STEPS)) for b in range(4)]
              + ["%s%d" % (n, i) for n in ("zy", "cy", "st") for i in range(len(Y_PARTS))]
              + ["%s%d" % (n, k) for n in ("hop", "arr") for k in range(len(PIECES))])


def bits(mask):
    return [b for b in range(mask.bit_length()) if (mask >> b) & 1]


def to_mask(engines):
    return sum(1 << b for b in engines)


def plan(T, topo):
    root = T.cores[T.root]
    away = [c for c in T.cores if topo.chip(c) != topo.chip(root)]
    home = [c for c in T.cores if topo.chip(c) == topo.chip(root) and c != root]
    own = [c for c in range(SIM_CORES) if c != root and topo.chip(c) == topo.chip(root)
           and all(topo.may_write(c, d) for d in away)]
    own.sort(key=lambda c: (T.rank_of(c) is None, c))
    far = [c for c in own if topo.die(c) != topo.die(root)]
    near = [c for c in own if topo.die(c) == topo.die(root)]
    return [far[0], near[0], far[1], near[1]], away, home


def view(T, p):
    v = T[p[0]][:, p[1]:p[2]]
    return v.bitcast(dt.uint8) if p[0] == "hq" else v


def transfer(T, topo, p, cores, mask, sem):
    ids = [DstId(rid=topo.addr(c)[0], pnc=topo.addr(c)[1]) for c in cores]
    return RemoteDMATransfer(dst_ids=ids, dma_engine_mask=mask, remote_sem=sem, srcs=[view(T, p)],
                             dsts=[view(T, p) for c in cores])


def root_masks(T, topo):
    root = T.cores[T.root]
    eng = bits(topo.mask(root, plan(T, topo)[0][0]))
    return [to_mask(eng[i::len(call)]) for call in SENDS for i in range(len(call))]


def relay_masks(T, topo):
    relay, away, home = plan(T, topo)
    out = topo.mask(relay[0], away[0])
    return out, topo.mask(relay[0], T.cores[T.root]) & ~out


def second_layer(g, T, needs, stores):
    S = T.sem
    g.tensor.wait_ge(S.qw2, 1)
    for i, (a, b) in enumerate(Y_PARTS):
        for s, n in needs(a, b):
            g.tensor.wait_ge(s, n)
        o = 512 * (4 + i)
        g.tensor.matmul_mx(T.ps[:, o:o + b - a], T.w2q[:, 0:128], T.w2s[:, 0:128],
                           T.hq[:, a:b], T.hs[:, a:b], True, True).then_inc(S["zy%d" % i], 1)
        k = [j for j, (u, v) in enumerate(stores) if u <= a and b <= v][0]
        if i % 2 == 0:
            g.vector.wait_ge(S["zy%d" % i], 1)
            g.vector.tensor_copy(T.yb[:, a:b], T.ps[:, o:o + b - a]).then_inc(S["cy%d" % k], 1)
        else:
            g.scalar.wait_ge(S["zy%d" % i], 1)
            g.scalar.activation(T.yb[:, a:b], T.ps[:, o:o + b - a],
                                ActivationFunctionType.Copy).then_inc(S["cy%d" % k], 1)
    for k, (u, v) in enumerate(stores):
        g.sync.wait_ge(S["cy%d" % k], len([1 for a, b in Y_PARTS if u <= a and b <= v]))
        g.sync.dma_start(T.y[:, u:v], T.yb[:, u:v]).then_inc(S["st%d" % k], 16)
    for k in range(len(stores)):
        g.sync.wait_ge(S["st%d" % k], 16)


def root_program(g, core, T, topo):
    S = T.sem
    g.sync.dma_start(T.w1b[:, :], T.w1[:, :]).then_inc(S.lw1, 16)
    for s, (a, b) in enumerate(STEPS):
        q = g.scalar if s in (0, 2) else g.sync
        q.dma_start(T.xb[:, 4 * a:4 * b], T.x[:, 4 * a:4 * b]).then_inc(S["lx%d" % s], 16)
    g.sync.dma_start(T.w2b[:, :], T.w2[:, :]).then_inc(S.lw2, 16)

    def bank(s, b):
        return 512 * (4 * (s % 2) + b)

    def quant_x(s):
        a, b = STEPS[s]
        g.vector.wait_ge(S["lx%d" % s], 16)
        g.vector.quantize_mx(T.xq[:, a:b], T.xs[:, a:b], T.xb[:, 4 * a:4 * b]).then_inc(S["qx%d" % s], 1)

    for s, (a, e) in enumerate(STEPS):
        g.tensor.wait_ge(S["qx%d" % s], 1)
        if s >= 2:
            g.tensor.wait_ge(S["act%d" % (s - 2)], 4)
        for b in range(4):
            if s == 0 and b == 0:
                g.tensor.wait_ge(S.qwa, 1)
            if s == 0 and b == 2:
                g.tensor.wait_ge(S.qwb, 1)
            o = bank(s, b)
            g.tensor.matmul_mx(T.ps[:, o:o + e - a], T.w1q[:, 128 * b:128 * b + 128], T.w1s[:, 128 * b:128 * b + 128],
                               T.xq[:, a:e], T.xs[:, a:e], True, True).then_inc(S["z%d%d" % (s, b)], 1)

    for s, (a, e) in enumerate(STEPS):
        for b in range(4):
            if b not in ON_VECTOR[s]:
                o = bank(s, b)
                g.scalar.wait_ge(S["z%d%d" % (s, b)], 1)
                g.scalar.activation(T.hb[:, 4 * a + b:4 * e:4], T.ps[:, o:o + e - a], ActivationFunctionType.Relu,
                                    scale=SCALE).then_inc(S["act%d" % s], 1)

    g.vector.wait_ge(S.lw1, 16)
    g.vector.quantize_mx(T.w1q[:, 0:256], T.w1s[:, 0:256], T.w1b[:, 0:1024]).then_inc(S.qwa, 1)
    g.vector.quantize_mx(T.w1q[:, 256:512], T.w1s[:, 256:512], T.w1b[:, 1024:2048]).then_inc(S.qwb, 1)
    quant_x(0)
    quant_x(1)
    for s, (a, e) in enumerate(STEPS):
        for b in ON_VECTOR[s]:
            o = bank(s, b)
            g.vector.wait_ge(S["z%d%d" % (s, b)], 1)
            g.vector.tensor_scalar(T.hb[:, 4 * a + b:4 * e:4], T.ps[:, o:o + e - a], 0.0, SCALE,
                                   AluOpType.max, AluOpType.mult).then_inc(S["act%d" % s], 1)
        g.vector.wait_ge(S["act%d" % s], 4)
        g.vector.quantize_mx(T.hq[:, a:e], T.hs[:, a:e], T.hb[:, 4 * a:4 * e]).then_inc(S["qh%d" % s], 1)
        if s + 2 < len(STEPS):
            quant_x(s + 2)
    g.vector.wait_ge(S.lw2, 16)
    g.vector.quantize_mx(T.w2q[:, 0:128], T.w2s[:, 0:128], T.w2b[:, 0:512]).then_inc(S.qw2, 1)

    relay, away, home = plan(T, topo)
    masks = root_masks(T, topo)
    packed = 0
    k = 0
    for call in SENDS:
        last = max(p[2] for p in call)
        while packed < len(STEPS) and STEPS[packed][0] < last:
            g.wait_ge(S["qh%d" % packed], 1)
            packed += 1
        parts = []
        for p in call:
            if p[3] is None:
                parts.append(transfer(T, topo, p, home, masks[k], S["arr%d" % k]))
            else:
                parts.append(transfer(T, topo, p, [relay[p[3]]], masks[k], S["hop%d" % k]))
            k += 1
        g.remote_dma_fused(parts, local_sem=S.sent)
    g.wait_ge(S.sent, sum(len(bits(m)) for m in masks))

    second_layer(g, T, lambda a, b: [(S["%s%d" % (n, s)], c) for s in range(len(STEPS)) for n, c in (("qh", 1), ("act", 4))],
                 Y_WHOLE)


def rank_program(g, core, T, topo):
    root = T.cores[T.root]
    if core == root:
        root_program(g, core, T, topo)
        return
    S = T.sem
    relay, away, home = plan(T, topo)
    masks = root_masks(T, topo)
    out, rest = relay_masks(T, topo)
    rank = T.rank_of(core)

    if rank is not None:
        g.sync.dma_start(T.w2b[:, :], T.w2[:, :]).then_inc(S.lw2, 16)
        g.vector.wait_ge(S.lw2, 16)
        g.vector.quantize_mx(T.w2q[:, 0:128], T.w2s[:, 0:128], T.w2b[:, 0:512]).then_inc(S.qw2, 1)

    if core in relay:
        sent = 0
        for k, p in enumerate(PIECES):
            if p[3] is None or relay[p[3]] != core:
                continue
            g.wait_ge(S["hop%d" % k], len(bits(masks[k])))
            there = [away[d] for d in p[4] if d != HOME]
            here = [c for c in home if c != core] if HOME in p[4] else []
            for cores, mask in ((there, out), (here, rest)):
                if cores:
                    g.remote_dma_fused([transfer(T, topo, p, cores, mask, S["arr%d" % k])], local_sem=S.sent)
                    sent += len(bits(mask))
        g.wait_ge(S.sent, sent)

    if rank is not None:
        def needs(a, b):
            r = []
            for k, p in enumerate(PIECES):
                if p[1] >= b or p[2] <= a:
                    continue
                if p[3] is not None and relay[p[3]] == core:
                    if HOME in p[4]:
                        r.append((S["hop%d" % k], len(bits(masks[k]))))
                elif core in away and away.index(core) in p[4]:
                    r.append((S["arr%d" % k], len(bits(out))))
                elif core in home and HOME in p[4]:
                    r.append((S["arr%d" % k], len(bits(masks[k] if p[3] is None else rest))))
            return r
        second_layer(g, T, needs, Y_WHOLE if core in relay else Y_EARLY)
